import numpy as np
import ml_dtypes


def mxq(x, axis, fmt="e4m3"):
    dtype, down = {"e4m3": (ml_dtypes.float8_e4m3fn, 7), "e5m2": (ml_dtypes.float8_e5m2, 14)}[fmt]
    v = np.moveaxis(np.asarray(x, np.float32).astype(ml_dtypes.bfloat16).astype(np.float64), axis, -1)
    blocks = v.reshape(v.shape[:-1] + (-1, 32))
    amax = np.abs(blocks).max(-1, keepdims=True)
    byte = np.maximum(np.where(amax > 0, np.frexp(amax)[1] - 1 + 127, 0) - down, 1)
    scale = np.exp2(byte - 127.0)
    codes = (blocks / scale).astype(np.float32).astype(dtype).astype(np.float64)
    return np.moveaxis((codes * scale).reshape(v.shape), -1, axis)


WIDE = False


def mx_kscale(k):
    if not WIDE:
        return np.ones(k)
    levels = np.array([10, -10, 5, -5, 0])
    if k % 512:
        return np.exp2(np.random.permutation(np.resize(levels, k // 32))).repeat(32)
    a = np.empty((k // 512, 16))
    for p in range(k // 512):
        a[p, :8] = np.random.permutation(np.resize(levels, 8))
        for g in range(8):
            far = levels[np.abs(levels - a[p, g]) >= 10]
            a[p, g + 8] = far[np.random.randint(len(far))]
    return np.exp2(a.ravel()).repeat(32)


BF16 = ml_dtypes.bfloat16


def bf(x):
    return np.asarray(x, np.float32).astype(BF16)


def f64(x):
    return np.asarray(x).astype(np.float64)


N, D, F, E = 4096, 1024, 512, 128


def modrelu_scale(zr, zi, b):
    m = np.sqrt(zr * zr + zi * zi + 1e-6)
    return np.maximum(m + b[None, :], 0.0) / m


def draw0():
    s, t = mx_kscale(D), mx_kscale(F)
    return {"x": bf(np.random.standard_normal((N, D)) * s),
            "wr": bf(np.random.standard_normal((D, F)) / np.sqrt(D) / s[:, None]),
            "wi": bf(np.random.standard_normal((D, F)) / np.sqrt(D) / s[:, None]),
            "b": bf(-0.5 + 0.3 * np.random.standard_normal(F)),
            "g": bf((1.0 + 0.1 * np.random.standard_normal(F)) * t),
            "vr": bf(np.random.standard_normal((F, E)) / np.sqrt(F) / t[:, None]),
            "vi": bf(np.random.standard_normal((F, E)) / np.sqrt(F) / t[:, None])}


def core(x, wr, wi, b, g, vr, vi):
    xq = mxq(f64(x), 1, "e4m3")
    zr = xq @ mxq(f64(wr), 0, "e4m3")
    zi = xq @ mxq(f64(wi), 0, "e4m3")
    sc = modrelu_scale(zr, zi, f64(b))
    gain = f64(g)[None, :]
    hr = mxq((sc * zr) * gain, 1, "e4m3")
    hi = mxq((sc * zi) * gain, 1, "e4m3")
    vrq = mxq(f64(vr), 0, "e4m3")
    viq = mxq(f64(vi), 0, "e4m3")
    yr = (hr @ vrq) - (hi @ viq)
    yi = (hr @ viq) + (hi @ vrq)
    return yr, yi


def e4m3fn_bytes(y):
    return np.clip(np.asarray(y, np.float64), -448.0, 448.0).astype(np.float32).astype(ml_dtypes.float8_e4m3fn).view(np.uint8)


def e4m3fn_values(b):
    return np.asarray(b, np.uint8).view(ml_dtypes.float8_e4m3fn).astype(np.float64)


def setup_inputs():
    d = draw0()
    x0 = np.asarray(d['x']).astype(np.float64)
    s = (np.max(np.abs(x0), axis=(0,), keepdims=True) / 448.0).astype(np.float32)
    out = {}
    for k, v in d.items():
        if k == 'x':
            out['x_bytes'] = e4m3fn_bytes(x0 / s.astype(np.float64))
            out['x_scale'] = s
        else:
            out[k] = v
    return out


def reference(x_bytes, x_scale, wr, wi, b, g, vr, vi):
    return core(e4m3fn_values(x_bytes) * x_scale.astype(np.float64), wr, wi, b, g, vr, vi)

from contextlib import ExitStack

import concourse.mybir as mybir
from concourse.masks import make_identity

N, D, F, E = 4096, 1024, 512, 128
FLOPS = 2 * N * D * F * 2 + 2 * N * F * E * 4

F32 = mybir.dt.float32
BF16 = mybir.dt.bfloat16
U32 = mybir.dt.uint32
U8 = mybir.dt.uint8
FP8 = mybir.dt.float8_e4m3fn
FP8X4 = mybir.dt.float8_e4m3fn_x4
ALU = mybir.AluOpType
ACT = mybir.ActivationFunctionType

P = 128
TILES = N // P
PAIRS = TILES // 2
G = D // 512
EPS = 1e-6


def tile_complexdensemodrelupair_t_kernel(tc, x_bytes, x_scale, wr, wi, b, g, vr, vi, out_r, out_i):
    nc = tc.nc
    x_rows = x_bytes.rearrange("(p i) k -> p (i k)", p=P)
    y_rows = [out_r.rearrange("(p i) e -> p i e", p=P), out_i.rearrange("(p i) e -> p i e", p=P)]

    with ExitStack() as ctx:
        keep = ctx.enter_context(tc.tile_pool(name="keep", bufs=1))
        xin = ctx.enter_context(tc.tile_pool(name="xin", bufs=3))
        xw = ctx.enter_context(tc.tile_pool(name="xw", bufs=3))
        hid = ctx.enter_context(tc.tile_pool(name="hid", bufs=3))
        outp = ctx.enter_context(tc.tile_pool(name="outp", bufs=3))
        mix_ps = ctx.enter_context(tc.psum_pool(name="mix_ps", bufs=2))
        z_ps = ctx.enter_context(tc.psum_pool(name="z_ps", bufs=6))

        x8 = {}

        def load_x(first, count):
            name = "x8_" + str(first)
            x8_part = keep.tile([P, count * D], U8, name=name)
            nc.sync.dma_start(out=x8_part[:], in_=x_rows[:, first * D:(first + count) * D])
            for i in range(count):
                x8[first + i] = x8_part[:, i * D:(i + 1) * D]

        w_raw = {}

        def load_w(which, src, gg):
            name = "w_raw_" + which + str(gg)
            w_part = keep.tile([P, 4, F], BF16, name=name)
            nc.sync.dma_start(out=w_part[:], in_=src[gg * 512:(gg + 1) * 512, :].rearrange("(p j) c -> p j c", j=4))
            w_raw[which, gg] = w_part

        load_x(0, 2)
        xs = keep.tile([P, G, 4], F32)
        nc.sync.dma_start(out=xs[:], in_=x_scale.rearrange("o (q p t) -> p (o q) t", p=P, t=4))
        load_w("r", wr, 0)
        load_w("r", wr, 1)
        load_x(2, 2)
        load_w("i", wi, 0)
        load_w("i", wi, 1)
        b_bf = keep.tile([P, 4], BF16)
        nc.sync.dma_start(out=b_bf[:], in_=b.rearrange("(p t) -> p t", t=4))
        g_bf = keep.tile([P, 4], BF16)
        nc.sync.dma_start(out=g_bf[:], in_=g.rearrange("(p t) -> p t", t=4))
        vr_raw = keep.tile([P, 4, E], BF16)
        nc.sync.dma_start(out=vr_raw[:], in_=vr.rearrange("(p j) e -> p j e", j=4))
        vi_raw = keep.tile([P, 4, E], BF16)
        nc.sync.dma_start(out=vi_raw[:], in_=vi.rearrange("(p j) e -> p j e", j=4))
        for first in range(4, TILES, 4):
            load_x(first, 4)

        warm = keep.tile([P, 1], F32)
        nc.vector.memset(warm[:], 1.0)
        nc.scalar.activation(out=warm[:], in_=warm[:], func=ACT.Abs_reciprocal_sqrt)
        ident = keep.tile([P, P], F32)
        make_identity(nc, ident[:])

        xb = {}

        def cast_x(i):
            if i % 2 == 0:
                xb_pair = xin.tile([P, 2 * D], BF16)
                xb[i // 2] = xb_pair
            nc.scalar.copy(out=xb[i // 2][:, (i % 2) * D:(i % 2 + 1) * D], in_=x8[i].bitcast(FP8))

        xt = {}

        def turn_x(q, gg):
            words = xb[q][:].bitcast(F32)
            bank = mix_ps.tile([P, 2, 256], F32, tag="mix")
            for h in range(2):
                for u in range(2):
                    first = h * 512 + 256 * gg
                    nc.tensor.transpose(bank[:, u, h * P:(h + 1) * P], words[:, first + u:first + 256:2], ident[:])
            xt[q, gg] = bank

        xg = {}

        def scale_x(q, gg):
            if gg == 0:
                xg_pair = xw.tile([P, G, 256, 4], BF16, align_bytes=64)
                xg[q] = xg_pair
            nc.vector.tensor_tensor(
                out=xg[q][:, gg, :, :].rearrange("p n (u e) -> p n u e", u=2),
                in0=xt[q, gg][:].bitcast(BF16).rearrange("p u (n e) -> p n u e", e=2),
                in1=xs[:, gg:gg + 1, :].to_broadcast([P, 256, 4]).rearrange("p n (u e) -> p n u e", u=2),
                op=ALU.mult,
            )

        xc = {}

        def quant_x(q):
            x_codes = xw.tile([P, G, 256], U32, align_bytes=64)
            x_sc = xw.tile([P, G, 256], U8, align_bytes=64)
            nc.vector.quantize_mx(
                out=x_codes[:].rearrange("p q n -> p (q n)").bitcast(FP8X4),
                scales=x_sc[:].rearrange("p q n -> p (q n)"),
                in_=xg[q][:].rearrange("p q n t -> p (q n t)"),
            )
            xc[q] = (x_codes, x_sc)

        w_grp = {}
        wc = {}

        def group_w(which, gg, how):
            name = "w_grp_" + which + str(gg)
            w_grouped = keep.tile([P, 4 * F], BF16, align_bytes=64, name=name)
            dst = w_grouped[:].rearrange("p (t m j) -> p t m j", t=4, j=4)
            src = w_raw[which, gg][:].rearrange("p j (m t) -> p t m j", t=4)
            for t in range(4):
                if how == "v":
                    nc.vector.tensor_copy(out=dst[:, t], in_=src[:, t])
                elif how == "s":
                    nc.scalar.copy(out=dst[:, t], in_=src[:, t])
                else:
                    nc.gpsimd.tensor_scalar(out=dst[:, t], in0=src[:, t], scalar1=1.0, scalar2=0.0, op0=ALU.mult, op1=ALU.add)
            w_grp[which, gg] = w_grouped

        def quant_w(which, gg):
            w_codes = keep.tile([P, F], U32, align_bytes=64, name="w_codes_" + which + str(gg))
            w_sc = keep.tile([P, F], U8, align_bytes=64, name="w_sc_" + which + str(gg))
            nc.vector.quantize_mx(out=w_codes[:].bitcast(FP8X4), scales=w_sc[:], in_=w_grp[which, gg][:])
            wc[which, gg] = (w_codes, w_sc)

        z = {}

        def dense_1(i, which):
            bank = z_ps.tile([P, 4, P], F32)
            x_codes, x_sc = xc[i // 2]
            cols = slice((i % 2) * P, (i % 2 + 1) * P)
            for t in range(4):
                for gg in range(G):
                    w_codes, w_sc = wc[which, gg]
                    rows = slice(t * P, (t + 1) * P)
                    nc.tensor.matmul_mx(
                        out=bank[:, t, :],
                        lhsT=w_codes[:, rows].bitcast(FP8X4),
                        lhsT_scale=w_sc[:, rows],
                        rhs=x_codes[:, gg, cols].bitcast(FP8X4),
                        rhs_scale=x_sc[:, gg, cols],
                        start=(gg == 0),
                        stop=(gg == G - 1),
                    )
            z[i, which] = bank

        sq = {}

        def squares(i):
            sq_pair = hid.tile([P, 2, 512], F32)
            nc.scalar.activation(out=sq_pair[:, 0, :], in_=z[i, "r"][:].rearrange("p t n -> p (t n)"), func=ACT.Square)
            nc.scalar.activation(out=sq_pair[:, 1, :], in_=z[i, "i"][:].rearrange("p t n -> p (t n)"), func=ACT.Square)
            sq[i] = sq_pair

        m2 = {}

        def add_squares(i):
            m2_tile = hid.tile([P, 512], F32)
            nc.gpsimd.tensor_tensor(out=m2_tile[:], in0=sq[i][:, 0, :], in1=sq[i][:, 1, :], op=ALU.add)
            m2[i] = m2_tile

        rs = {}

        def rsqrt(i):
            r_tile = hid.tile([P, 4, P], F32)
            nc.scalar.activation(out=r_tile[:].rearrange("p t n -> p (t n)"), in_=m2[i][:], func=ACT.Abs_reciprocal_sqrt, bias=EPS)
            rs[i] = r_tile

        gain = {}

        def affine(i):
            gain_tile = hid.tile([P, 4, P], F32)
            for t in range(4):
                nc.scalar.activation(
                    out=gain_tile[:, t, :], in_=rs[i][:, t, :], func=ACT.Relu, scale=beta[:, t:t + 1], bias=absg[:, t:t + 1],
                )
            gain[i] = gain_tile

        h = {}

        def hidden(i):
            h_tile = hid.tile([P, 2, P, 4], BF16, align_bytes=64)
            for o, which in ((0, "r"), (1, "i")):
                nc.vector.tensor_tensor(
                    out=h_tile[:, o, :, :].rearrange("p (c k) t -> p c t k", k=4),
                    in0=z[i, which][:].rearrange("p t (c k) -> p c t k", k=4),
                    in1=gain[i][:].rearrange("p t (c k) -> p c t k", k=4),
                    op=ALU.mult,
                )
            h[i] = h_tile

        hc = {}

        def quant_h(i):
            h_codes = hid.tile([P, 2 * P], U32, align_bytes=64)
            h_sc = hid.tile([P, 2 * P], U8, align_bytes=64)
            nc.vector.quantize_mx(out=h_codes[:].bitcast(FP8X4), scales=h_sc[:], in_=h[i][:].rearrange("p o n t -> p (o n t)"))
            hc[i] = (h_codes, h_sc)

        y = {}

        def dense_2(i):
            if i % 2 == 0:
                y_bank = mix_ps.tile([P, 2, 2 * E], F32, tag="mix")
                y[i // 2] = y_bank
            h_codes, h_sc = hc[i]
            for o in range(2):
                rows = slice(o * P, (o + 1) * P)
                cols = slice((1 - o) * E, (3 - o) * E)
                nc.tensor.matmul_mx(
                    out=y[i // 2][:, i % 2, :],
                    lhsT=h_codes[:, rows].bitcast(FP8X4),
                    lhsT_scale=h_sc[:, rows],
                    rhs=v_codes[:, cols].bitcast(FP8X4),
                    rhs_scale=v_sc[:, cols],
                    start=(o == 0),
                    stop=(o == 1),
                )

        ysb = {}

        def emit_y(q):
            if q % 2 == 0:
                y_tile = outp.tile([P, 2, 4, E], F32)
                ysb[q // 2] = y_tile
            half = (q % 2) * 2
            nc.scalar.copy(
                out=ysb[q // 2][:, :, half:half + 2, :],
                in_=y[q][:].rearrange("p j (o e) -> p o j e", o=2),
            )
            if q % 2 == 1:
                for o in range(2):
                    nc.sync.dma_start(out=y_rows[o][:, 2 * q - 2:2 * q + 2, :], in_=ysb[q // 2][:, o, :, :])

        sgn = keep.tile([P, 4], F32)
        nsgn = keep.tile([P, 4], F32)
        absg = keep.tile([P, 4], F32)
        beta = keep.tile([P, 4], F32)
        v_grp = keep.tile([P, 3, E, 4], BF16, align_bytes=64)
        v_codes = keep.tile([P, 3 * E], U32, align_bytes=64)
        v_sc = keep.tile([P, 3 * E], U8, align_bytes=64)

        def prep_v():
            step_g = keep.tile([P, 4], F32)
            nc.gpsimd.tensor_scalar(out=step_g[:], in0=g_bf[:], scalar1=0.0, scalar2=2.0, op0=ALU.is_ge, op1=ALU.mult)
            nc.gpsimd.tensor_scalar(out=sgn[:], in0=step_g[:], scalar1=1.0, scalar2=-1.0, op0=ALU.mult, op1=ALU.add)
            nc.gpsimd.tensor_scalar(out=nsgn[:], in0=step_g[:], scalar1=-1.0, scalar2=1.0, op0=ALU.mult, op1=ALU.add)
            nc.gpsimd.tensor_tensor(out=absg[:], in0=g_bf[:], in1=sgn[:], op=ALU.mult)
            nc.gpsimd.tensor_tensor(out=beta[:], in0=absg[:], in1=b_bf[:], op=ALU.mult)
            for o, raw, s in ((0, vi_raw, nsgn), (1, vr_raw, sgn), (2, vi_raw, sgn)):
                nc.gpsimd.tensor_tensor(
                    out=v_grp[:, o, :, :], in0=raw[:].rearrange("p j e -> p e j"),
                    in1=s[:].unsqueeze(1).to_broadcast([P, E, 4]), op=ALU.mult,
                )

        def quant_v():
            for o in range(3):
                cols = slice(o * E, (o + 1) * E)
                nc.vector.quantize_mx(
                    out=v_codes[:, cols].bitcast(FP8X4), scales=v_sc[:, cols],
                    in_=v_grp[:, o, :, :].rearrange("p e j -> p (e j)"),
                )

        for s in range(-6, TILES + 4):
            if s == -4:
                group_w("r", 0, "v")
                quant_w("r", 0)
                group_w("r", 1, "g")
            if s == -2:
                quant_w("r", 1)
                group_w("i", 0, "g")
                group_w("i", 1, "v")
                prep_v()
            if s == 0:
                quant_w("i", 1)
                quant_w("i", 0)
            if s == 1:
                quant_v()
            if 0 <= (s + 4) // 2 < PAIRS and s % 2 == 0:
                turn_x((s + 4) // 2, 0)
            if 0 <= (s + 3) // 2 < PAIRS and s % 2 == 1:
                turn_x((s + 3) // 2, 1)
            if s % 2 == 1 and 0 <= (s + 3) // 2 < PAIRS:
                scale_x((s + 3) // 2, 0)
            if s % 2 == 0 and 0 <= (s + 2) // 2 < PAIRS:
                scale_x((s + 2) // 2, 1)
            if 0 <= s - 2 < TILES:
                hidden(s - 2)
            if 0 <= s - 3 < TILES:
                quant_h(s - 3)
            if s % 2 == 0 and 0 <= (s + 2) // 2 < PAIRS:
                quant_x((s + 2) // 2)
            if 0 <= s < TILES:
                dense_1(s, "r")
                dense_1(s, "i")
                squares(s)
                add_squares(s)
            if 0 <= s - 1 < TILES:
                rsqrt(s - 1)
                affine(s - 1)
            if 0 <= s + 6 < TILES:
                cast_x(s + 6)
            if s % 2 == 1 and 0 <= (s - 5) // 2 < PAIRS:
                dense_2(s - 5)
                dense_2(s - 4)
                emit_y((s - 5) // 2)
